import numpy as np
import ml_dtypes


def mxq(x, axis, fmt="e4m3"):
    dtype, down = {"e4m3": (ml_dtypes.float8_e4m3fn, 7), "e5m2": (ml_dtypes.float8_e5m2, 14)}[fmt]
    v = np.moveaxis(np.asarray(x, np.float32).astype(ml_dtypes.bfloat16).astype(np.float64), axis, -1)
    blocks = v.reshape(v.shape[:-1] + (-1, 32))
    amax = np.abs(blocks).max(-1, keepdims=True)
    byte = np.maximum(np.where(amax > 0, np.frexp(amax)[1] - 1 + 127, 0) - down, 1)
    scale = np.exp2(byte - 127.0)
    codes = (blocks / scale).astype(np.float32).astype(dtype).astype(np.float64)
    return np.moveaxis((codes * scale).reshape(v.shape), -1, axis)


WIDE = False


def mx_kscale(k):
    if not WIDE:
        return np.ones(k)
    levels = np.array([10, -10, 5, -5, 0])
    if k % 512:
        return np.exp2(np.random.permutation(np.resize(levels, k // 32))).repeat(32)
    a = np.empty((k // 512, 16))
    for p in range(k // 512):
        a[p, :8] = np.random.permutation(np.resize(levels, 8))
        for g in range(8):
            far = levels[np.abs(levels - a[p, g]) >= 10]
            a[p, g + 8] = far[np.random.randint(len(far))]
    return np.exp2(a.ravel()).repeat(32)


def f64(x):
    return np.asarray(x).astype(np.float64)


E2M1 = np.array([0.0, 0.5, 1.0, 1.5, 2.0, 3.0, 4.0, 6.0, -0.0, -0.5, -1.0, -1.5, -2.0, -3.0, -4.0, -6.0])


def pack_weight(w, fmt):
    k, n = w.shape
    w = f64(np.asarray(w, np.float32).astype(ml_dtypes.bfloat16)).reshape(k // 32, 32, n)
    amax = np.abs(w).max(1)
    if fmt == "e4m3":
        byte = np.frexp(amax)[1] - 1 + 127 - 7
    else:
        mant, ex = np.frexp(amax / 6.0)
        byte = np.where(mant > 0.5, ex, ex - 1) + 127
    byte = np.clip(np.where(amax > 0, byte, 1), 1, 254)
    scaled = (w * np.exp2(127.0 - byte)[:, None, :]).reshape(k, n).astype(np.float32)
    by_word = np.ascontiguousarray(scaled.reshape(k // 512, 128, 4, n).transpose(0, 1, 3, 2))
    if fmt == "e4m3":
        words = by_word.astype(ml_dtypes.float8_e4m3fn).view(np.uint8)
    else:
        c = by_word.astype(ml_dtypes.float4_e2m1fn).view(np.uint8) & 0xF
        words = (c[..., 0::2] | (c[..., 1::2] << 4)).reshape(k // 512, 128, 2 * n)
    return np.ascontiguousarray(words), np.ascontiguousarray(byte.astype(np.uint8).reshape(k // 512, 16, n))


def unpack_weight(words, scales, fmt):
    g, _, n = scales.shape
    words = np.ascontiguousarray(words).reshape(g, 128, n, -1)
    if fmt == "e4m3":
        vals = words.view(ml_dtypes.float8_e4m3fn).astype(np.float64)
    else:
        nib = np.empty((g, 128, n, 4), np.uint8)
        nib[..., 0::2] = words & 0xF
        nib[..., 1::2] = words >> 4
        vals = E2M1[nib]
    vals = vals * np.repeat(np.exp2(scales.astype(np.float64) - 127.0), 8, axis=1)[..., None]
    return vals.transpose(0, 1, 3, 2).reshape(g * 512, n)


def bf(x):
    return np.asarray(x, np.float32).astype(ml_dtypes.bfloat16)


def planes(Y):
    r, m = Y.shape
    b = f64(bf(Y)).reshape(r // 32, 32, m)
    amax = np.abs(b).max(1)
    byte = np.clip(np.where(amax > 0, np.frexp(amax)[1] - 1 + 127 - 7, 1), 1, 254)
    codes = (b * np.exp2(127.0 - byte)[:, None, :]).reshape(r, m).astype(np.float32).astype(ml_dtypes.float8_e4m3fn).view(np.uint8)
    words = codes.reshape(r // 512, 128, 4, m).transpose(0, 1, 3, 2)
    return np.ascontiguousarray(words), np.ascontiguousarray(byte.astype(np.uint8).reshape(r // 512, 16, m))


K, L, T, N = 1024, 512, 512, 512


def setup_inputs():
    n = np.random.standard_normal
    fk = mx_kscale(K)
    fl = mx_kscale(L)
    wap = pack_weight(n((K, N)) * 1 / np.sqrt(K) * fk[:, None], "e2m1")
    xqp = pack_weight(n((L, T)) / fl[:, None], "e4m3")
    wsp = pack_weight(n((L, N)) * 1 / np.sqrt(L) * fl[:, None], "e2m1")
    wcp = pack_weight(n((K, N)) * 1 / np.sqrt(K) * fk[:, None], "e4m3")
    return {
        "xt": (n((K, T)) / fk[:, None]).astype(np.float32),
        "wa_words": wap[0],
        "wa_scales": wap[1],
        "xq_words": xqp[0],
        "xq_scales": xqp[1],
        "ws_words": wsp[0],
        "ws_scales": wsp[1],
        "wc_words": wcp[0],
        "wc_scales": wcp[1],
        "bi": (np.random.uniform(-1.0, 1.0, (1, N))).astype(np.float32),
    }


def reference(xt, wa_words, wa_scales, xq_words, xq_scales, ws_words, ws_scales, wc_words, wc_scales, bi):
    wau = unpack_weight(wa_words, wa_scales, "e2m1")
    xqu = unpack_weight(xq_words, xq_scales, "e4m3")
    wsu = unpack_weight(ws_words, ws_scales, "e2m1")
    wcu = unpack_weight(wc_words, wc_scales, "e4m3")
    xtq = mxq(f64(xt), 0, "e4m3")
    a0 = xtq.T @ wau + xqu.T @ wsu
    b0 = xtq.T @ wcu
    a = a0 + f64(bi)
    b = b0 + f64(bi)
    y = a - b * np.mean(a * b, axis=1, keepdims=True) / (np.mean(np.square(b), axis=1, keepdims=True) + 0.1)
    words, scales = planes(y)
    return y, words, scales

@@ -1,0 +1,239 @@
+from contextlib import ExitStack
+
+import concourse.mybir as mybir
+from concourse.masks import make_identity
+
+K, L, T, N = 1024, 512, 512, 512
+FLOPS = 2 * T * N * (K + L + K)
+
+F32 = mybir.dt.float32
+BF16 = mybir.dt.bfloat16
+I32 = mybir.dt.int32
+U32 = mybir.dt.uint32
+U8 = mybir.dt.uint8
+FP8X4 = mybir.dt.float8_e4m3fn_x4
+FP4X4 = mybir.dt.float4_e2m1fn_x4
+ALU = mybir.AluOpType
+ACT = mybir.ActivationFunctionType
+
+P = 128
+PACK = 4
+QUADS = 4
+HALF = T // 2
+EPS_SUM = N * 0.1
+
+
+def tile_mix_rows_less_common_part_pl_kernel(
+    tc, xt, wa_words, wa_scales, xq_words, xq_scales, ws_words, ws_scales, wc_words, wc_scales, bi, out_0, out_1, out_2
+):
+    nc = tc.nc
+    with ExitStack() as ctx:
+        sb = ctx.enter_context(tc.tile_pool(name="sb", bufs=1))
+        ps = ctx.enter_context(tc.psum_pool(name="ps", bufs=1))
+        ctx.enter_context(tc.manual_schedule())
+
+        bias_col = sb.tile([P, PACK], F32)
+        ident = sb.tile([P, P], F32)
+        bias = sb.tile([P, N], F32)
+        x0 = sb.tile([P, PACK, T], F32)
+        x1 = [sb.tile([P, PACK, HALF], F32, name="x1_%d" % h) for h in range(2)]
+        xb = [sb.tile([P, PACK, P, PACK], BF16, name="xb%d" % g, align_bytes=64) for g in range(2)]
+        xc = [sb.tile([P, T], U32, name="xc%d" % g, align_bytes=64) for g in range(2)]
+        xs = [sb.tile([P, T], U8, name="xs%d" % g, align_bytes=64) for g in range(2)]
+        wc = [sb.tile([P, N], U32, name="wc%d" % g, align_bytes=64) for g in range(2)]
+        wcs = sb.tile([P, N], U8, align_bytes=64)
+        wa = sb.tile([P, 2, 2 * N], U8, align_bytes=64)
+        was = sb.tile([P, 2, N], U8, align_bytes=64)
+        ws = sb.tile([P, 2 * N], U8, align_bytes=64)
+        wss = sb.tile([P, N], U8, align_bytes=64)
+        xq_in = sb.tile([P, T], U32, align_bytes=64)
+        xqs_in = sb.tile([P, T], U8, align_bytes=64)
+        xq = sb.tile([P, T], U32, align_bytes=64)
+        xqs = sb.tile([P, T], U8, align_bytes=64)
+        a = [sb.tile([P, N], F32, name="a%d" % r) for r in range(PACK)]
+        b = [sb.tile([P, N], F32, name="b%d" % r) for r in range(PACK)]
+        y = sb.tile([P, PACK, N], F32)
+        yb = sb.tile([P, N, PACK], BF16, align_bytes=64)
+        yc = sb.tile([P, N], U32, align_bytes=64)
+        ys = sb.tile([P, N], U8, align_bytes=64)
+        squares = sb.tile([P, N], F32)
+        products = sb.tile([P, N], F32)
+        bb = sb.tile([P, PACK], F32)
+        den = sb.tile([P, PACK], F32)
+        rec = sb.tile([P, PACK], F32)
+        coef = sb.tile([P, PACK], F32)
+
+        for plane in (wcs[:], xqs_in[:], was[:].rearrange("p g n -> p (g n)"), wss[:]):
+            nc.vector.memset(plane.bitcast(I32), 0)
+
+        make_identity(nc, ident[:])
+
+        def rows(g):
+            return xt[g * P * PACK : (g + 1) * P * PACK, :].rearrange("(p j) t -> p j t", j=PACK)
+
+        def words(ap):
+            return ap.rearrange("p n j -> p (n j)").bitcast(I32)
+
+        def scale_rows(queue, plane, src):
+            for q in range(QUADS):
+                queue.dma_start(
+                    out=plane[32 * q : 32 * q + 4, :].bitcast(I32), in_=src[0, 4 * q : 4 * q + 4, :].bitcast(I32)
+                )
+
+        nc.sync.dma_start(out=x0[:], in_=rows(0))
+        nc.sync.dma_start(out=bias_col[:], in_=bi.rearrange("o (p j) -> (o p) j", j=PACK))
+        for q in range(QUADS):
+            nc.sync.dma_start(
+                out=wcs[32 * q + 4 : 32 * q + 12, :].bitcast(I32), in_=wc_scales[:, 4 * q : 4 * q + 4, :].bitcast(I32)
+            )
+        nc.sync.dma_start(out=wc[0][:].bitcast(I32), in_=words(wc_words[0]))
+        for h in range(2):
+            nc.sync.dma_start(out=x1[h][:], in_=rows(1)[:, :, h * HALF : (h + 1) * HALF])
+        for q in range(QUADS):
+            nc.sync.dma_start(
+                out=was[32 * q : 32 * q + 4, :, :].bitcast(I32),
+                in_=wa_scales[:, 4 * q : 4 * q + 4, :].rearrange("g r n -> r g n").bitcast(I32),
+            )
+        nc.sync.dma_start(out=wc[1][:].bitcast(I32), in_=words(wc_words[1]))
+        nc.sync.dma_start(out=xq_in[:].bitcast(I32), in_=words(xq_words[0]))
+        nc.sync.dma_start(out=wa[:].bitcast(I32), in_=wa_words.rearrange("g p n -> p g n").bitcast(I32))
+        nc.sync.dma_start(out=ws[:].bitcast(I32), in_=ws_words[0].bitcast(I32))
+        scale_rows(nc.sync, wss, ws_scales)
+        scale_rows(nc.gpsimd, xqs_in, xq_scales)
+
+        bias_ps = ps.tile([P, PACK, P], F32, tag="a3")
+        for j in range(PACK):
+            nc.tensor.transpose(bias_ps[:, j, :], bias_col[:, j : j + 1].to_broadcast([P, P]), ident[:])
+
+        def scalar_copy(out, in_):
+            nc.scalar.activation(out=out, in_=in_, func=ACT.Copy)
+
+        def cast_x(copy, g, raw, first, m0, m1):
+            copy(
+                out=xb[g][:, :, m0:m1, :].rearrange("p r m j -> p m j r"),
+                in_=raw[:].rearrange("p j (m r) -> p m j r", r=PACK)[:, m0 - first : m1 - first, :, :],
+            )
+
+        def quantize_x(g, r):
+            cols = slice(r * P, (r + 1) * P)
+            nc.vector.quantize_mx(
+                out=xc[g][:, cols].bitcast(FP8X4), scales=xs[g][:, cols], in_=xb[g][:, r, :, :].rearrange("p m j -> p (m j)")
+            )
+
+        cast_x(nc.vector.tensor_copy, 0, x0, 0, 0, 84)
+        cast_x(scalar_copy, 0, x0, 0, 84, 128)
+        scalar_copy(bias[:].rearrange("p (k j) -> p k j", j=PACK), bias_ps[:].rearrange("p j k -> p k j"))
+
+        b_ps = [ps.tile([P, N], F32, name="b_ps%d" % r, tag="b%d" % r) for r in range(PACK)]
+        a_ps = [ps.tile([P, N], F32, name="a_ps%d" % r, tag="a%d" % r) for r in range(PACK)]
+
+        def b_pass(g, r):
+            cols = slice(r * P, (r + 1) * P)
+            nc.tensor.matmul_mx(
+                out=b_ps[r][:], lhsT=xc[g][:, cols].bitcast(FP8X4), lhsT_scale=xs[g][:, cols],
+                rhs=wc[g][:].bitcast(FP8X4), rhs_scale=wcs[4 + 4 * g : P, :], start=(g == 0), stop=(g == 1),
+            )
+
+        def a_passes(r):
+            cols = slice(r * P, (r + 1) * P)
+            for g in range(2):
+                nc.tensor.matmul_mx(
+                    out=a_ps[r][:], lhsT=xc[g][:, cols].bitcast(FP8X4), lhsT_scale=xs[g][:, cols],
+                    rhs=wa[:, g, :].bitcast(FP4X4), rhs_scale=was[:, g, :], start=(g == 0), stop=False,
+                )
+            nc.tensor.matmul_mx(
+                out=a_ps[r][:], lhsT=xq[:, cols].bitcast(FP8X4), lhsT_scale=xqs[:, cols],
+                rhs=ws[:].bitcast(FP4X4), rhs_scale=wss[:], start=False, stop=True,
+            )
+
+        for r in range(PACK):
+            quantize_x(0, r)
+            b_pass(0, r)
+        nc.vector.tensor_copy(
+            out=xqs[:].rearrange("p (r m) -> p r m", r=PACK), in_=xqs_in[:].rearrange("p (m r) -> p r m", r=PACK)
+        )
+        cast_x(nc.vector.tensor_copy, 1, x1[0], 0, 0, 44)
+        cast_x(scalar_copy, 1, x1[0], 0, 44, 64)
+        cast_x(nc.vector.tensor_copy, 1, x1[1], 64, 64, 108)
+        cast_x(scalar_copy, 1, x1[1], 64, 108, 128)
+        for r in range(PACK):
+            quantize_x(1, r)
+            b_pass(1, r)
+        for r in range(PACK):
+            nc.gpsimd.tensor_copy(out=xq[:, r * P : (r + 1) * P], in_=xq_in[:, r:T:PACK])
+            a_passes(r)
+
+        def add_b(r):
+            nc.vector.tensor_tensor(out=b[r][:], in0=b_ps[r][:], in1=bias[:], op=ALU.add)
+            nc.scalar.activation(out=squares[:], in_=b[r][:], func=ACT.Square, accum_out=bb[:, r : r + 1])
+
+        def denominator(r0):
+            nc.scalar.activation(out=den[:, r0 : r0 + 2], in_=bb[:, r0 : r0 + 2], func=ACT.Copy, scale=-1.0, bias=-EPS_SUM)
+
+        def invert(r0):
+            nc.vector.reciprocal(out=rec[:, r0 : r0 + 2], in_=den[:, r0 : r0 + 2])
+
+        def add_a(r):
+            nc.vector.tensor_tensor(out=a[r][:], in0=a_ps[r][:], in1=bias[:], op=ALU.add)
+
+        def project(r):
+            nc.vector.scalar_tensor_tensor(
+                out=products[:], in0=a[r][:], scalar=rec[:, r : r + 1], in1=b[r][:], op0=ALU.mult, op1=ALU.mult,
+                accum_out=coef[:, r : r + 1],
+            )
+
+        def subtract(r, c0, c1):
+            nc.vector.scalar_tensor_tensor(
+                out=y[:, r, c0:c1], in0=b[r][:, c0:c1], scalar=coef[:, r : r + 1], in1=a[r][:, c0:c1],
+                op0=ALU.mult, op1=ALU.add,
+            )
+
+        out_rows = out_0.rearrange("(p r) n -> p r n", r=PACK)
+
+        def store_y(r):
+            nc.sync.dma_start(out=out_rows[:, r, :], in_=y[:, r, :])
+
+        def cast_y(copy, c0, c1):
+            copy(
+                out=yb[:, c0:c1, :].rearrange("p (c i) r -> p c r i", i=4),
+                in_=y[:, :, c0:c1].rearrange("p r (c i) -> p c r i", i=4),
+            )
+
+        add_b(0)
+        add_b(1)
+        denominator(0)
+        add_b(2)
+        add_b(3)
+        denominator(2)
+        invert(0)
+        add_a(0)
+        add_a(1)
+        invert(2)
+        project(0)
+        add_a(2)
+        project(1)
+        add_a(3)
+        subtract(0, 0, N)
+        store_y(0)
+        project(2)
+        subtract(1, 0, N)
+        store_y(1)
+        project(3)
+        subtract(2, 0, N)
+        store_y(2)
+        subtract(3, 0, N // 2)
+        subtract(3, N // 2, N)
+        store_y(3)
+        cast_y(scalar_copy, 0, 192)
+        cast_y(nc.vector.tensor_copy, 192, 256)
+        cast_y(nc.vector.tensor_copy, 256, N)
+        codes_out = words(out_1[0])
+        for h in range(2):
+            cols = slice(h * N // 2, (h + 1) * N // 2)
+            nc.vector.quantize_mx(
+                out=yc[:, cols].bitcast(FP8X4), scales=ys[:, cols], in_=yb[:, cols, :].rearrange("p n r -> p (n r)")
+            )
+            nc.sync.dma_start(out=codes_out[:, cols], in_=yc[:, cols].bitcast(I32))
+        for q in range(QUADS):
+            queue = nc.scalar if q % 2 else nc.sync
+            queue.dma_start(out=out_2[0, 4 * q : 4 * q + 4, :].bitcast(I32), in_=ys[32 * q : 32 * q + 4, :].bitcast(I32))

@@ -19,7 +19,6 @@ ACT = mybir.ActivationFunctionType
 P = 128
 PACK = 4
 QUADS = 4
-HALF = T // 2
 EPS_SUM = N * 0.1
 
 
@@ -35,14 +34,13 @@ def tile_mix_rows_less_common_part_pl_kernel(
         bias_col = sb.tile([P, PACK], F32)
         ident = sb.tile([P, P], F32)
         bias = sb.tile([P, N], F32)
-        x0 = sb.tile([P, PACK, T], F32)
-        x1 = [sb.tile([P, PACK, HALF], F32, name="x1_%d" % h) for h in range(2)]
+        x = [sb.tile([P, PACK, T], F32, name="x%d" % g) for g in range(2)]
         xb = [sb.tile([P, PACK, P, PACK], BF16, name="xb%d" % g, align_bytes=64) for g in range(2)]
         xc = [sb.tile([P, T], U32, name="xc%d" % g, align_bytes=64) for g in range(2)]
         xs = [sb.tile([P, T], U8, name="xs%d" % g, align_bytes=64) for g in range(2)]
         wc = [sb.tile([P, N], U32, name="wc%d" % g, align_bytes=64) for g in range(2)]
         wcs = sb.tile([P, N], U8, align_bytes=64)
-        wa = sb.tile([P, 2, 2 * N], U8, align_bytes=64)
+        wa = [sb.tile([P, 2 * N], U8, name="wa%d" % g, align_bytes=64) for g in range(2)]
         was = sb.tile([P, 2, N], U8, align_bytes=64)
         ws = sb.tile([P, 2 * N], U8, align_bytes=64)
         wss = sb.tile([P, N], U8, align_bytes=64)
@@ -63,7 +61,7 @@ def tile_mix_rows_less_common_part_pl_kernel(
         rec = sb.tile([P, PACK], F32)
         coef = sb.tile([P, PACK], F32)
 
-        for plane in (wcs[:], xqs_in[:], was[:].rearrange("p g n -> p (g n)"), wss[:]):
+        for plane in (was[:].rearrange("p g n -> p (g n)"), xqs_in[:], wcs[:], wss[:]):
             nc.vector.memset(plane.bitcast(I32), 0)
 
         make_identity(nc, ident[:])
@@ -80,23 +78,23 @@ def tile_mix_rows_less_common_part_pl_kernel(
                     out=plane[32 * q : 32 * q + 4, :].bitcast(I32), in_=src[0, 4 * q : 4 * q + 4, :].bitcast(I32)
                 )
 
-        nc.sync.dma_start(out=x0[:], in_=rows(0))
+        nc.sync.dma_start(out=x[0][:], in_=rows(0))
         nc.sync.dma_start(out=bias_col[:], in_=bi.rearrange("o (p j) -> (o p) j", j=PACK))
-        for q in range(QUADS):
-            nc.sync.dma_start(
-                out=wcs[32 * q + 4 : 32 * q + 12, :].bitcast(I32), in_=wc_scales[:, 4 * q : 4 * q + 4, :].bitcast(I32)
-            )
-        nc.sync.dma_start(out=wc[0][:].bitcast(I32), in_=words(wc_words[0]))
-        for h in range(2):
-            nc.sync.dma_start(out=x1[h][:], in_=rows(1)[:, :, h * HALF : (h + 1) * HALF])
         for q in range(QUADS):
             nc.sync.dma_start(
                 out=was[32 * q : 32 * q + 4, :, :].bitcast(I32),
                 in_=wa_scales[:, 4 * q : 4 * q + 4, :].rearrange("g r n -> r g n").bitcast(I32),
             )
-        nc.sync.dma_start(out=wc[1][:].bitcast(I32), in_=words(wc_words[1]))
+        nc.sync.dma_start(out=wa[0][:].bitcast(I32), in_=wa_words[0].bitcast(I32))
+        nc.sync.dma_start(out=x[1][:], in_=rows(1))
+        for q in range(QUADS):
+            nc.sync.dma_start(
+                out=wcs[32 * q + 4 : 32 * q + 12, :].bitcast(I32), in_=wc_scales[:, 4 * q : 4 * q + 4, :].bitcast(I32)
+            )
+        for g in range(2):
+            nc.sync.dma_start(out=wc[g][:].bitcast(I32), in_=words(wc_words[g]))
+        nc.sync.dma_start(out=wa[1][:].bitcast(I32), in_=wa_words[1].bitcast(I32))
         nc.sync.dma_start(out=xq_in[:].bitcast(I32), in_=words(xq_words[0]))
-        nc.sync.dma_start(out=wa[:].bitcast(I32), in_=wa_words.rearrange("g p n -> p g n").bitcast(I32))
         nc.sync.dma_start(out=ws[:].bitcast(I32), in_=ws_words[0].bitcast(I32))
         scale_rows(nc.sync, wss, ws_scales)
         scale_rows(nc.gpsimd, xqs_in, xq_scales)
@@ -108,10 +106,10 @@ def tile_mix_rows_less_common_part_pl_kernel(
         def scalar_copy(out, in_):
             nc.scalar.activation(out=out, in_=in_, func=ACT.Copy)
 
-        def cast_x(copy, g, raw, first, m0, m1):
+        def cast_x(copy, g, m0, m1):
             copy(
                 out=xb[g][:, :, m0:m1, :].rearrange("p r m j -> p m j r"),
-                in_=raw[:].rearrange("p j (m r) -> p m j r", r=PACK)[:, m0 - first : m1 - first, :, :],
+                in_=x[g][:].rearrange("p j (m r) -> p m j r", r=PACK)[:, m0:m1, :, :],
             )
 
         def quantize_x(g, r):
@@ -120,8 +118,8 @@ def tile_mix_rows_less_common_part_pl_kernel(
                 out=xc[g][:, cols].bitcast(FP8X4), scales=xs[g][:, cols], in_=xb[g][:, r, :, :].rearrange("p m j -> p (m j)")
             )
 
-        cast_x(nc.vector.tensor_copy, 0, x0, 0, 0, 84)
-        cast_x(scalar_copy, 0, x0, 0, 84, 128)
+        cast_x(nc.vector.tensor_copy, 0, 0, 84)
+        cast_x(scalar_copy, 0, 84, P)
         scalar_copy(bias[:].rearrange("p (k j) -> p k j", j=PACK), bias_ps[:].rearrange("p j k -> p k j"))
 
         b_ps = [ps.tile([P, N], F32, name="b_ps%d" % r, tag="b%d" % r) for r in range(PACK)]
@@ -134,13 +132,15 @@ def tile_mix_rows_less_common_part_pl_kernel(
                 rhs=wc[g][:].bitcast(FP8X4), rhs_scale=wcs[4 + 4 * g : P, :], start=(g == 0), stop=(g == 1),
             )
 
-        def a_passes(r):
+        def a_pass(g, r):
             cols = slice(r * P, (r + 1) * P)
-            for g in range(2):
-                nc.tensor.matmul_mx(
-                    out=a_ps[r][:], lhsT=xc[g][:, cols].bitcast(FP8X4), lhsT_scale=xs[g][:, cols],
-                    rhs=wa[:, g, :].bitcast(FP4X4), rhs_scale=was[:, g, :], start=(g == 0), stop=False,
-                )
+            nc.tensor.matmul_mx(
+                out=a_ps[r][:], lhsT=xc[g][:, cols].bitcast(FP8X4), lhsT_scale=xs[g][:, cols],
+                rhs=wa[g][:].bitcast(FP4X4), rhs_scale=was[:, g, :], start=(g == 0), stop=False,
+            )
+
+        def s_pass(r):
+            cols = slice(r * P, (r + 1) * P)
             nc.tensor.matmul_mx(
                 out=a_ps[r][:], lhsT=xq[:, cols].bitcast(FP8X4), lhsT_scale=xqs[:, cols],
                 rhs=ws[:].bitcast(FP4X4), rhs_scale=wss[:], start=False, stop=True,
@@ -148,20 +148,20 @@ def tile_mix_rows_less_common_part_pl_kernel(
 
         for r in range(PACK):
             quantize_x(0, r)
-            b_pass(0, r)
-        nc.vector.tensor_copy(
-            out=xqs[:].rearrange("p (r m) -> p r m", r=PACK), in_=xqs_in[:].rearrange("p (m r) -> p r m", r=PACK)
-        )
-        cast_x(nc.vector.tensor_copy, 1, x1[0], 0, 0, 44)
-        cast_x(scalar_copy, 1, x1[0], 0, 44, 64)
-        cast_x(nc.vector.tensor_copy, 1, x1[1], 64, 64, 108)
-        cast_x(scalar_copy, 1, x1[1], 64, 108, 128)
+            a_pass(0, r)
+        cast_x(nc.vector.tensor_copy, 1, 0, 84)
+        cast_x(scalar_copy, 1, 84, P)
         for r in range(PACK):
             quantize_x(1, r)
-            b_pass(1, r)
+        for r0 in (0, 2):
+            for g in range(2):
+                b_pass(g, r0)
+                b_pass(g, r0 + 1)
         for r in range(PACK):
             nc.gpsimd.tensor_copy(out=xq[:, r * P : (r + 1) * P], in_=xq_in[:, r:T:PACK])
-            a_passes(r)
+            nc.gpsimd.tensor_copy(out=xqs[:, r * P : (r + 1) * P], in_=xqs_in[:, r:T:PACK])
+            a_pass(1, r)
+            s_pass(r)
 
         def add_b(r):
             nc.vector.tensor_tensor(out=b[r][:], in0=b_ps[r][:], in1=bias[:], op=ALU.add)
@@ -219,21 +219,24 @@ def tile_mix_rows_less_common_part_pl_kernel(
         subtract(1, 0, N)
         store_y(1)
         project(3)
-        subtract(2, 0, N)
-        store_y(2)
-        subtract(3, 0, N // 2)
-        subtract(3, N // 2, N)
-        store_y(3)
-        cast_y(scalar_copy, 0, 192)
-        cast_y(nc.vector.tensor_copy, 192, 256)
-        cast_y(nc.vector.tensor_copy, 256, N)
         codes_out = words(out_1[0])
-        for h in range(2):
-            cols = slice(h * N // 2, (h + 1) * N // 2)
+
+        def quantize_y(c0, c1):
             nc.vector.quantize_mx(
-                out=yc[:, cols].bitcast(FP8X4), scales=ys[:, cols], in_=yb[:, cols, :].rearrange("p n r -> p (n r)")
+                out=yc[:, c0:c1].bitcast(FP8X4), scales=ys[:, c0:c1], in_=yb[:, c0:c1, :].rearrange("p n r -> p (n r)")
             )
-            nc.sync.dma_start(out=codes_out[:, cols], in_=yc[:, cols].bitcast(I32))
+
+        for c0, c1 in ((0, 128), (128, 256), (256, N)):
+            subtract(2, c0, c1)
+            subtract(3, c0, c1)
+            cast_y(scalar_copy, c0, min(c1, 320))
+        nc.sync.dma_start(out=out_rows[:, 2:4, :], in_=y[:, 2:4, :])
+        quantize_y(0, 128)
+        cast_y(nc.vector.tensor_copy, 320, N)
+        quantize_y(128, 256)
+        nc.sync.dma_start(out=codes_out[:, 0:256], in_=yc[:, 0:256].bitcast(I32))
+        quantize_y(256, N)
+        nc.sync.dma_start(out=codes_out[:, 256:N], in_=yc[:, 256:N].bitcast(I32))
         for q in range(QUADS):
-            queue = nc.scalar if q % 2 else nc.sync
+            queue = nc.sync if q == QUADS - 1 else nc.scalar
             queue.dma_start(out=out_2[0, 4 * q : 4 * q + 4, :].bitcast(I32), in_=ys[32 * q : 32 * q + 4, :].bitcast(I32))

@@ -19,7 +19,13 @@ ACT = mybir.ActivationFunctionType
 P = 128
 PACK = 4
 QUADS = 4
+PASSES = K // (P * PACK)
 EPS_SUM = N * 0.1
+
+X_SPLIT = 84
+Y_RANGES = ((0, 128), (128, 256), (256, N))
+Y_SPLIT = 320
+HALF = N // 2
 
 
 def tile_mix_rows_less_common_part_pl_kernel(
@@ -34,14 +40,14 @@ def tile_mix_rows_less_common_part_pl_kernel(
         bias_col = sb.tile([P, PACK], F32)
         ident = sb.tile([P, P], F32)
         bias = sb.tile([P, N], F32)
-        x = [sb.tile([P, PACK, T], F32, name="x%d" % g) for g in range(2)]
-        xb = [sb.tile([P, PACK, P, PACK], BF16, name="xb%d" % g, align_bytes=64) for g in range(2)]
-        xc = [sb.tile([P, T], U32, name="xc%d" % g, align_bytes=64) for g in range(2)]
-        xs = [sb.tile([P, T], U8, name="xs%d" % g, align_bytes=64) for g in range(2)]
-        wc = [sb.tile([P, N], U32, name="wc%d" % g, align_bytes=64) for g in range(2)]
+        x = [sb.tile([P, PACK, T], F32, name="x%d" % g) for g in range(PASSES)]
+        xb = [sb.tile([P, PACK, P, PACK], BF16, name="xb%d" % g, align_bytes=64) for g in range(PASSES)]
+        xc = [sb.tile([P, T], U32, name="xc%d" % g, align_bytes=64) for g in range(PASSES)]
+        xs = [sb.tile([P, T], U8, name="xs%d" % g, align_bytes=64) for g in range(PASSES)]
+        wc = [sb.tile([P, N], U32, name="wc%d" % g, align_bytes=64) for g in range(PASSES)]
         wcs = sb.tile([P, N], U8, align_bytes=64)
-        wa = [sb.tile([P, 2 * N], U8, name="wa%d" % g, align_bytes=64) for g in range(2)]
-        was = sb.tile([P, 2, N], U8, align_bytes=64)
+        wa = [sb.tile([P, 2 * N], U8, name="wa%d" % g, align_bytes=64) for g in range(PASSES)]
+        was = sb.tile([P, PASSES, N], U8, align_bytes=64)
         ws = sb.tile([P, 2 * N], U8, align_bytes=64)
         wss = sb.tile([P, N], U8, align_bytes=64)
         xq_in = sb.tile([P, T], U32, align_bytes=64)
@@ -54,8 +60,7 @@ def tile_mix_rows_less_common_part_pl_kernel(
         yb = sb.tile([P, N, PACK], BF16, align_bytes=64)
         yc = sb.tile([P, N], U32, align_bytes=64)
         ys = sb.tile([P, N], U8, align_bytes=64)
-        squares = sb.tile([P, N], F32)
-        products = sb.tile([P, N], F32)
+        squares = sb.tile([P, PACK, N], F32)
         bb = sb.tile([P, PACK], F32)
         den = sb.tile([P, PACK], F32)
         rec = sb.tile([P, PACK], F32)
@@ -63,7 +68,6 @@ def tile_mix_rows_less_common_part_pl_kernel(
 
         for plane in (was[:].rearrange("p g n -> p (g n)"), xqs_in[:], wcs[:], wss[:]):
             nc.vector.memset(plane.bitcast(I32), 0)
-
         make_identity(nc, ident[:])
 
         def rows(g):
@@ -91,7 +95,7 @@ def tile_mix_rows_less_common_part_pl_kernel(
             nc.sync.dma_start(
                 out=wcs[32 * q + 4 : 32 * q + 12, :].bitcast(I32), in_=wc_scales[:, 4 * q : 4 * q + 4, :].bitcast(I32)
             )
-        for g in range(2):
+        for g in range(PASSES):
             nc.sync.dma_start(out=wc[g][:].bitcast(I32), in_=words(wc_words[g]))
         nc.sync.dma_start(out=wa[1][:].bitcast(I32), in_=wa_words[1].bitcast(I32))
         nc.sync.dma_start(out=xq_in[:].bitcast(I32), in_=words(xq_words[0]))
@@ -106,10 +110,10 @@ def tile_mix_rows_less_common_part_pl_kernel(
         def scalar_copy(out, in_):
             nc.scalar.activation(out=out, in_=in_, func=ACT.Copy)
 
-        def cast_x(copy, g, m0, m1):
+        def round_x(copy, g, m0, m1):
             copy(
-                out=xb[g][:, :, m0:m1, :].rearrange("p r m j -> p m j r"),
-                in_=x[g][:].rearrange("p j (m r) -> p m j r", r=PACK)[:, m0:m1, :, :],
+                out=xb[g][:, :, m0:m1, :].rearrange("p r m j -> p m r j"),
+                in_=x[g][:].rearrange("p j (m r) -> p m r j", r=PACK)[:, m0:m1, :, :],
             )
 
         def quantize_x(g, r):
@@ -118,28 +122,28 @@ def tile_mix_rows_less_common_part_pl_kernel(
                 out=xc[g][:, cols].bitcast(FP8X4), scales=xs[g][:, cols], in_=xb[g][:, r, :, :].rearrange("p m j -> p (m j)")
             )
 
-        cast_x(nc.vector.tensor_copy, 0, 0, 84)
-        cast_x(scalar_copy, 0, 84, P)
-        scalar_copy(bias[:].rearrange("p (k j) -> p k j", j=PACK), bias_ps[:].rearrange("p j k -> p k j"))
+        round_x(nc.vector.tensor_copy, 0, 0, X_SPLIT)
+        round_x(scalar_copy, 0, X_SPLIT, P)
+        scalar_copy(bias[:].rearrange("p (i j) -> p i j", j=PACK), bias_ps[:].rearrange("p j i -> p i j"))
 
         b_ps = [ps.tile([P, N], F32, name="b_ps%d" % r, tag="b%d" % r) for r in range(PACK)]
         a_ps = [ps.tile([P, N], F32, name="a_ps%d" % r, tag="a%d" % r) for r in range(PACK)]
 
-        def b_pass(g, r):
+        def wc_pass(g, r):
             cols = slice(r * P, (r + 1) * P)
             nc.tensor.matmul_mx(
                 out=b_ps[r][:], lhsT=xc[g][:, cols].bitcast(FP8X4), lhsT_scale=xs[g][:, cols],
-                rhs=wc[g][:].bitcast(FP8X4), rhs_scale=wcs[4 + 4 * g : P, :], start=(g == 0), stop=(g == 1),
+                rhs=wc[g][:].bitcast(FP8X4), rhs_scale=wcs[4 + 4 * g : P, :], start=(g == 0), stop=(g == PASSES - 1),
             )
 
-        def a_pass(g, r):
+        def wa_pass(g, r):
             cols = slice(r * P, (r + 1) * P)
             nc.tensor.matmul_mx(
                 out=a_ps[r][:], lhsT=xc[g][:, cols].bitcast(FP8X4), lhsT_scale=xs[g][:, cols],
                 rhs=wa[g][:].bitcast(FP4X4), rhs_scale=was[:, g, :], start=(g == 0), stop=False,
             )
 
-        def s_pass(r):
+        def ws_pass(r):
             cols = slice(r * P, (r + 1) * P)
             nc.tensor.matmul_mx(
                 out=a_ps[r][:], lhsT=xq[:, cols].bitcast(FP8X4), lhsT_scale=xqs[:, cols],
@@ -148,24 +152,23 @@ def tile_mix_rows_less_common_part_pl_kernel(
 
         for r in range(PACK):
             quantize_x(0, r)
-            a_pass(0, r)
-        cast_x(nc.vector.tensor_copy, 1, 0, 84)
-        cast_x(scalar_copy, 1, 84, P)
+            wa_pass(0, r)
+        round_x(nc.vector.tensor_copy, 1, 0, X_SPLIT)
+        round_x(scalar_copy, 1, X_SPLIT, P)
         for r in range(PACK):
             quantize_x(1, r)
-        for r0 in (0, 2):
-            for g in range(2):
-                b_pass(g, r0)
-                b_pass(g, r0 + 1)
+        for r in range(PACK):
+            wc_pass(0, r)
+            wc_pass(1, r)
         for r in range(PACK):
             nc.gpsimd.tensor_copy(out=xq[:, r * P : (r + 1) * P], in_=xq_in[:, r:T:PACK])
             nc.gpsimd.tensor_copy(out=xqs[:, r * P : (r + 1) * P], in_=xqs_in[:, r:T:PACK])
-            a_pass(1, r)
-            s_pass(r)
+            wa_pass(1, r)
+            ws_pass(r)
 
         def add_b(r):
             nc.vector.tensor_tensor(out=b[r][:], in0=b_ps[r][:], in1=bias[:], op=ALU.add)
-            nc.scalar.activation(out=squares[:], in_=b[r][:], func=ACT.Square, accum_out=bb[:, r : r + 1])
+            nc.scalar.activation(out=squares[:, r, :], in_=b[r][:], func=ACT.Square, accum_out=bb[:, r : r + 1])
 
         def denominator(r0):
             nc.scalar.activation(out=den[:, r0 : r0 + 2], in_=bb[:, r0 : r0 + 2], func=ACT.Copy, scale=-1.0, bias=-EPS_SUM)
@@ -178,7 +181,7 @@ def tile_mix_rows_less_common_part_pl_kernel(
 
         def project(r):
             nc.vector.scalar_tensor_tensor(
-                out=products[:], in0=a[r][:], scalar=rec[:, r : r + 1], in1=b[r][:], op0=ALU.mult, op1=ALU.mult,
+                out=y[:, r, :], in0=a[r][:], scalar=rec[:, r : r + 1], in1=b[r][:], op0=ALU.mult, op1=ALU.mult,
                 accum_out=coef[:, r : r + 1],
             )
 
@@ -193,18 +196,26 @@ def tile_mix_rows_less_common_part_pl_kernel(
         def store_y(r):
             nc.sync.dma_start(out=out_rows[:, r, :], in_=y[:, r, :])
 
-        def cast_y(copy, c0, c1):
+        def round_y(copy, c0, c1):
             copy(
                 out=yb[:, c0:c1, :].rearrange("p (c i) r -> p c r i", i=4),
                 in_=y[:, :, c0:c1].rearrange("p r (c i) -> p c r i", i=4),
             )
 
-        add_b(0)
-        add_b(1)
-        denominator(0)
-        add_b(2)
-        add_b(3)
-        denominator(2)
+        codes_out = words(out_1[0])
+
+        def quantize_y(c0, c1):
+            nc.vector.quantize_mx(
+                out=yc[:, c0:c1].bitcast(FP8X4), scales=ys[:, c0:c1], in_=yb[:, c0:c1, :].rearrange("p n r -> p (n r)")
+            )
+
+        def store_codes(c0, c1):
+            nc.sync.dma_start(out=codes_out[:, c0:c1], in_=yc[:, c0:c1].bitcast(I32))
+
+        for r in range(PACK):
+            add_b(r)
+            if r % 2:
+                denominator(r - 1)
         invert(0)
         add_a(0)
         add_a(1)
@@ -216,27 +227,22 @@ def tile_mix_rows_less_common_part_pl_kernel(
         subtract(0, 0, N)
         store_y(0)
         project(2)
+        project(3)
         subtract(1, 0, N)
         store_y(1)
-        project(3)
-        codes_out = words(out_1[0])
 
-        def quantize_y(c0, c1):
-            nc.vector.quantize_mx(
-                out=yc[:, c0:c1].bitcast(FP8X4), scales=ys[:, c0:c1], in_=yb[:, c0:c1, :].rearrange("p n r -> p (n r)")
-            )
-
-        for c0, c1 in ((0, 128), (128, 256), (256, N)):
+        for c0, c1 in Y_RANGES:
             subtract(2, c0, c1)
             subtract(3, c0, c1)
-            cast_y(scalar_copy, c0, min(c1, 320))
-        nc.sync.dma_start(out=out_rows[:, 2:4, :], in_=y[:, 2:4, :])
-        quantize_y(0, 128)
-        cast_y(nc.vector.tensor_copy, 320, N)
-        quantize_y(128, 256)
-        nc.sync.dma_start(out=codes_out[:, 0:256], in_=yc[:, 0:256].bitcast(I32))
-        quantize_y(256, N)
-        nc.sync.dma_start(out=codes_out[:, 256:N], in_=yc[:, 256:N].bitcast(I32))
+            round_y(scalar_copy, c0, min(c1, Y_SPLIT))
+            if c1 % HALF == 0:
+                nc.sync.dma_start(out=out_rows[:, 2:4, c1 - HALF : c1], in_=y[:, 2:4, c1 - HALF : c1])
+        quantize_y(*Y_RANGES[0])
+        round_y(nc.vector.tensor_copy, Y_SPLIT, N)
+        quantize_y(*Y_RANGES[1])
+        store_codes(0, HALF)
+        quantize_y(*Y_RANGES[2])
+        store_codes(HALF, N)
         for q in range(QUADS):
             queue = nc.sync if q == QUADS - 1 else nc.scalar
             queue.dma_start(out=out_2[0, 4 * q : 4 * q + 4, :].bitcast(I32), in_=ys[32 * q : 32 * q + 4, :].bitcast(I32))

from contextlib import ExitStack

import concourse.mybir as mybir
from concourse.masks import make_identity

K, L, T, N = 1024, 512, 512, 512
FLOPS = 2 * T * N * (K + L + K)

F32 = mybir.dt.float32
BF16 = mybir.dt.bfloat16
I32 = mybir.dt.int32
U32 = mybir.dt.uint32
U8 = mybir.dt.uint8
FP8X4 = mybir.dt.float8_e4m3fn_x4
FP4X4 = mybir.dt.float4_e2m1fn_x4
ALU = mybir.AluOpType
ACT = mybir.ActivationFunctionType

P = 128
PACK = 4
QUADS = 4
PASSES = K // (P * PACK)
EPS_SUM = N * 0.1

X_SPLIT = 84
Y_RANGES = ((0, 128), (128, 256), (256, N))
Y_SPLIT = 320
HALF = N // 2


def tile_mix_rows_less_common_part_pl_kernel(
    tc, xt, wa_words, wa_scales, xq_words, xq_scales, ws_words, ws_scales, wc_words, wc_scales, bi, out_0, out_1, out_2
):
    nc = tc.nc
    with ExitStack() as ctx:
        sb = ctx.enter_context(tc.tile_pool(name="sb", bufs=1))
        ps = ctx.enter_context(tc.psum_pool(name="ps", bufs=1))
        ctx.enter_context(tc.manual_schedule())

        bias_col = sb.tile([P, PACK], F32)
        ident = sb.tile([P, P], F32)
        bias = sb.tile([P, N], F32)
        x = [sb.tile([P, PACK, T], F32, name="x%d" % g) for g in range(PASSES)]
        xb = [sb.tile([P, PACK, P, PACK], BF16, name="xb%d" % g, align_bytes=64) for g in range(PASSES)]
        xc = [sb.tile([P, T], U32, name="xc%d" % g, align_bytes=64) for g in range(PASSES)]
        xs = [sb.tile([P, T], U8, name="xs%d" % g, align_bytes=64) for g in range(PASSES)]
        wc = [sb.tile([P, N], U32, name="wc%d" % g, align_bytes=64) for g in range(PASSES)]
        wcs = sb.tile([P, N], U8, align_bytes=64)
        wa = [sb.tile([P, 2 * N], U8, name="wa%d" % g, align_bytes=64) for g in range(PASSES)]
        was = sb.tile([P, PASSES, N], U8, align_bytes=64)
        ws = sb.tile([P, 2 * N], U8, align_bytes=64)
        wss = sb.tile([P, N], U8, align_bytes=64)
        xq_in = sb.tile([P, T], U32, align_bytes=64)
        xqs_in = sb.tile([P, T], U8, align_bytes=64)
        xq = sb.tile([P, T], U32, align_bytes=64)
        xqs = sb.tile([P, T], U8, align_bytes=64)
        a = [sb.tile([P, N], F32, name="a%d" % r) for r in range(PACK)]
        b = [sb.tile([P, N], F32, name="b%d" % r) for r in range(PACK)]
        y = sb.tile([P, PACK, N], F32)
        yb = sb.tile([P, N, PACK], BF16, align_bytes=64)
        yc = sb.tile([P, N], U32, align_bytes=64)
        ys = sb.tile([P, N], U8, align_bytes=64)
        squares = sb.tile([P, PACK, N], F32)
        bb = sb.tile([P, PACK], F32)
        den = sb.tile([P, PACK], F32)
        rec = sb.tile([P, PACK], F32)
        coef = sb.tile([P, PACK], F32)

        for plane in (was[:].rearrange("p g n -> p (g n)"), xqs_in[:], wcs[:], wss[:]):
            nc.vector.memset(plane.bitcast(I32), 0)
        make_identity(nc, ident[:])

        def rows(g):
            return xt[g * P * PACK : (g + 1) * P * PACK, :].rearrange("(p j) t -> p j t", j=PACK)

        def words(ap):
            return ap.rearrange("p n j -> p (n j)").bitcast(I32)

        def scale_rows(queue, plane, src):
            for q in range(QUADS):
                queue.dma_start(
                    out=plane[32 * q : 32 * q + 4, :].bitcast(I32), in_=src[0, 4 * q : 4 * q + 4, :].bitcast(I32)
                )

        nc.sync.dma_start(out=x[0][:], in_=rows(0))
        nc.sync.dma_start(out=bias_col[:], in_=bi.rearrange("o (p j) -> (o p) j", j=PACK))
        for q in range(QUADS):
            nc.sync.dma_start(
                out=was[32 * q : 32 * q + 4, :, :].bitcast(I32),
                in_=wa_scales[:, 4 * q : 4 * q + 4, :].rearrange("g r n -> r g n").bitcast(I32),
            )
        nc.sync.dma_start(out=wa[0][:].bitcast(I32), in_=wa_words[0].bitcast(I32))
        nc.sync.dma_start(out=x[1][:], in_=rows(1))
        for q in range(QUADS):
            nc.sync.dma_start(
                out=wcs[32 * q + 4 : 32 * q + 12, :].bitcast(I32), in_=wc_scales[:, 4 * q : 4 * q + 4, :].bitcast(I32)
            )
        for g in range(PASSES):
            nc.sync.dma_start(out=wc[g][:].bitcast(I32), in_=words(wc_words[g]))
        nc.sync.dma_start(out=wa[1][:].bitcast(I32), in_=wa_words[1].bitcast(I32))
        nc.sync.dma_start(out=xq_in[:].bitcast(I32), in_=words(xq_words[0]))
        nc.sync.dma_start(out=ws[:].bitcast(I32), in_=ws_words[0].bitcast(I32))
        scale_rows(nc.sync, wss, ws_scales)
        scale_rows(nc.gpsimd, xqs_in, xq_scales)

        bias_ps = ps.tile([P, PACK, P], F32, tag="a3")
        for j in range(PACK):
            nc.tensor.transpose(bias_ps[:, j, :], bias_col[:, j : j + 1].to_broadcast([P, P]), ident[:])

        def scalar_copy(out, in_):
            nc.scalar.activation(out=out, in_=in_, func=ACT.Copy)

        def round_x(copy, g, m0, m1):
            copy(
                out=xb[g][:, :, m0:m1, :].rearrange("p r m j -> p m r j"),
                in_=x[g][:].rearrange("p j (m r) -> p m r j", r=PACK)[:, m0:m1, :, :],
            )

        def quantize_x(g, r):
            cols = slice(r * P, (r + 1) * P)
            nc.vector.quantize_mx(
                out=xc[g][:, cols].bitcast(FP8X4), scales=xs[g][:, cols], in_=xb[g][:, r, :, :].rearrange("p m j -> p (m j)")
            )

        round_x(nc.vector.tensor_copy, 0, 0, X_SPLIT)
        round_x(scalar_copy, 0, X_SPLIT, P)
        scalar_copy(bias[:].rearrange("p (i j) -> p i j", j=PACK), bias_ps[:].rearrange("p j i -> p i j"))

        b_ps = [ps.tile([P, N], F32, name="b_ps%d" % r, tag="b%d" % r) for r in range(PACK)]
        a_ps = [ps.tile([P, N], F32, name="a_ps%d" % r, tag="a%d" % r) for r in range(PACK)]

        def wc_pass(g, r):
            cols = slice(r * P, (r + 1) * P)
            nc.tensor.matmul_mx(
                out=b_ps[r][:], lhsT=xc[g][:, cols].bitcast(FP8X4), lhsT_scale=xs[g][:, cols],
                rhs=wc[g][:].bitcast(FP8X4), rhs_scale=wcs[4 + 4 * g : P, :], start=(g == 0), stop=(g == PASSES - 1),
            )

        def wa_pass(g, r):
            cols = slice(r * P, (r + 1) * P)
            nc.tensor.matmul_mx(
                out=a_ps[r][:], lhsT=xc[g][:, cols].bitcast(FP8X4), lhsT_scale=xs[g][:, cols],
                rhs=wa[g][:].bitcast(FP4X4), rhs_scale=was[:, g, :], start=(g == 0), stop=False,
            )

        def ws_pass(r):
            cols = slice(r * P, (r + 1) * P)
            nc.tensor.matmul_mx(
                out=a_ps[r][:], lhsT=xq[:, cols].bitcast(FP8X4), lhsT_scale=xqs[:, cols],
                rhs=ws[:].bitcast(FP4X4), rhs_scale=wss[:], start=False, stop=True,
            )

        for r in range(PACK):
            quantize_x(0, r)
            wa_pass(0, r)
        round_x(nc.vector.tensor_copy, 1, 0, X_SPLIT)
        round_x(scalar_copy, 1, X_SPLIT, P)
        for r in range(PACK):
            quantize_x(1, r)
        for r in range(PACK):
            wc_pass(0, r)
            wc_pass(1, r)
        for r in range(PACK):
            nc.gpsimd.tensor_copy(out=xq[:, r * P : (r + 1) * P], in_=xq_in[:, r:T:PACK])
            nc.gpsimd.tensor_copy(out=xqs[:, r * P : (r + 1) * P], in_=xqs_in[:, r:T:PACK])
            wa_pass(1, r)
            ws_pass(r)

        def add_b(r):
            nc.vector.tensor_tensor(out=b[r][:], in0=b_ps[r][:], in1=bias[:], op=ALU.add)
            nc.scalar.activation(out=squares[:, r, :], in_=b[r][:], func=ACT.Square, accum_out=bb[:, r : r + 1])

        def denominator(r0):
            nc.scalar.activation(out=den[:, r0 : r0 + 2], in_=bb[:, r0 : r0 + 2], func=ACT.Copy, scale=-1.0, bias=-EPS_SUM)

        def invert(r0):
            nc.vector.reciprocal(out=rec[:, r0 : r0 + 2], in_=den[:, r0 : r0 + 2])

        def add_a(r):
            nc.vector.tensor_tensor(out=a[r][:], in0=a_ps[r][:], in1=bias[:], op=ALU.add)

        def project(r):
            nc.vector.scalar_tensor_tensor(
                out=y[:, r, :], in0=a[r][:], scalar=rec[:, r : r + 1], in1=b[r][:], op0=ALU.mult, op1=ALU.mult,
                accum_out=coef[:, r : r + 1],
            )

        def subtract(r, c0, c1):
            nc.vector.scalar_tensor_tensor(
                out=y[:, r, c0:c1], in0=b[r][:, c0:c1], scalar=coef[:, r : r + 1], in1=a[r][:, c0:c1],
                op0=ALU.mult, op1=ALU.add,
            )

        out_rows = out_0.rearrange("(p r) n -> p r n", r=PACK)

        def store_y(r):
            nc.sync.dma_start(out=out_rows[:, r, :], in_=y[:, r, :])

        def round_y(copy, c0, c1):
            copy(
                out=yb[:, c0:c1, :].rearrange("p (c i) r -> p c r i", i=4),
                in_=y[:, :, c0:c1].rearrange("p r (c i) -> p c r i", i=4),
            )

        codes_out = words(out_1[0])

        def quantize_y(c0, c1):
            nc.vector.quantize_mx(
                out=yc[:, c0:c1].bitcast(FP8X4), scales=ys[:, c0:c1], in_=yb[:, c0:c1, :].rearrange("p n r -> p (n r)")
            )

        def store_codes(c0, c1):
            nc.sync.dma_start(out=codes_out[:, c0:c1], in_=yc[:, c0:c1].bitcast(I32))

        for r in range(PACK):
            add_b(r)
            if r % 2:
                denominator(r - 1)
        invert(0)
        add_a(0)
        add_a(1)
        invert(2)
        project(0)
        add_a(2)
        project(1)
        add_a(3)
        subtract(0, 0, N)
        store_y(0)
        project(2)
        project(3)
        subtract(1, 0, N)
        store_y(1)

        for c0, c1 in Y_RANGES:
            subtract(2, c0, c1)
            subtract(3, c0, c1)
            round_y(scalar_copy, c0, min(c1, Y_SPLIT))
            if c1 % HALF == 0:
                nc.sync.dma_start(out=out_rows[:, 2:4, c1 - HALF : c1], in_=y[:, 2:4, c1 - HALF : c1])
        quantize_y(*Y_RANGES[0])
        round_y(nc.vector.tensor_copy, Y_SPLIT, N)
        quantize_y(*Y_RANGES[1])
        store_codes(0, HALF)
        quantize_y(*Y_RANGES[2])
        store_codes(HALF, N)
        for q in range(QUADS):
            queue = nc.sync if q == QUADS - 1 else nc.scalar
            queue.dma_start(out=out_2[0, 4 * q : 4 * q + 4, :].bitcast(I32), in_=ys[32 * q : 32 * q + 4, :].bitcast(I32))
